import numpy as np
import ml_dtypes


def mxq(x, axis, fmt="e4m3"):
    dtype, down = {"e4m3": (ml_dtypes.float8_e4m3fn, 7), "e5m2": (ml_dtypes.float8_e5m2, 14)}[fmt]
    v = np.moveaxis(np.asarray(x, np.float32).astype(ml_dtypes.bfloat16).astype(np.float64), axis, -1)
    blocks = v.reshape(v.shape[:-1] + (-1, 32))
    amax = np.abs(blocks).max(-1, keepdims=True)
    byte = np.maximum(np.where(amax > 0, np.frexp(amax)[1] - 1 + 127, 0) - down, 1)
    scale = np.exp2(byte - 127.0)
    codes = (blocks / scale).astype(np.float32).astype(dtype).astype(np.float64)
    return np.moveaxis((codes * scale).reshape(v.shape), -1, axis)


WIDE = False


def mx_kscale(k):
    if not WIDE:
        return np.ones(k)
    levels = np.array([10, -10, 5, -5, 0])
    if k % 512:
        return np.exp2(np.random.permutation(np.resize(levels, k // 32))).repeat(32)
    a = np.empty((k // 512, 16))
    for p in range(k // 512):
        a[p, :8] = np.random.permutation(np.resize(levels, 8))
        for g in range(8):
            far = levels[np.abs(levels - a[p, g]) >= 10]
            a[p, g + 8] = far[np.random.randint(len(far))]
    return np.exp2(a.ravel()).repeat(32)


def f64(x):
    return np.asarray(x).astype(np.float64)


def striped(idx):
    return np.tile(idx.reshape(-1, 16).T, (8, 1)).astype(np.uint16)


def unstriped(offs):
    return offs[:16].T.reshape(-1).astype(np.int64)


def striped8(idx):
    return np.concatenate([x.reshape(-1, 16).T for x in idx]).astype(np.uint16)


def runs(offs, k):
    lists = np.stack([offs[16 * r : 16 * r + 16].T.reshape(-1) for r in range(8)]).astype(np.int64)
    return lists[np.arange(k) % 512 // 64]


def pack_weight(w):
    k, n = w.shape
    w = f64(np.asarray(w, np.float32).astype(ml_dtypes.bfloat16)).reshape(k // 32, 32, n)
    amax = np.abs(w).max(1)
    byte = np.clip(np.where(amax > 0, np.frexp(amax)[1] - 1 + 127 - 7, 1), 1, 254)
    scaled = (w * np.exp2(127.0 - byte)[:, None, :]).reshape(k, n).astype(np.float32)
    words = np.ascontiguousarray(scaled.reshape(k // 512, 128, 4, n).transpose(0, 1, 3, 2)).astype(ml_dtypes.float8_e4m3fn).view(np.uint8)
    return words, np.ascontiguousarray(byte.astype(np.uint8).reshape(k // 512, 16, n))


def unpack_weight(words, scales):
    g, p, n, _ = words.shape
    vals = np.ascontiguousarray(words).view(ml_dtypes.float8_e4m3fn).astype(np.float64) * np.repeat(np.exp2(scales.astype(np.float64) - 127.0), 8, axis=1)[..., None]
    return vals.transpose(0, 1, 3, 2).reshape(g * 512, n)


K, T, S, H, G, U = 512, 2048, 256, 512, 2048, 512


def setup_inputs():
    n = np.random.standard_normal
    s = mx_kscale(K)[:, None]
    packed_xT = pack_weight(n((K, T)) * s)
    packed_dT = pack_weight(n((K, G)) / s)
    perm = np.random.permutation(U)
    return {
        "x_words": packed_xT[0],
        "x_scales": packed_xT[1],
        "w1": (n((K, H)) / np.sqrt(K) / s).astype(np.float32),
        "gs": (np.random.uniform(0.5, 1.5, (K, 1)) * s).astype(np.float32),
        "d_words": packed_dT[0],
        "d_scales": packed_dT[1],
        "offs": striped(np.random.permutation(T)[:S]),
        "n1": striped8(np.stack([np.random.permutation(S) for _ in range(8)])),
        "n2": striped8(np.stack([np.random.permutation(S) for _ in range(8)])),
        "ka": striped8(np.random.randint(0, G, (8, H))),
        "kb": striped8(np.random.randint(0, G, (8, H))),
        "n3": striped(perm[:S]),
        "n4": striped(perm[S:]),
        "n5": striped(np.random.permutation(U)),
    }


def reference(x_words, x_scales, w1, gs, d_words, d_scales, offs, n1, n2, ka, kb, n3, n4, n5):
    d_ka = unpack_weight(d_words, d_scales)[np.arange(K)[:, None], runs(ka, K)]
    xq = unpack_weight(x_words, x_scales)[:, unstriped(offs)]
    y = mxq(f64(w1), 0, "e4m3").T @ xq
    z = f64(gs) * (y - (np.minimum(y[np.arange(H)[:, None], runs(n1, H)], y[np.arange(H)[:, None], runs(n2, H)])))
    zq = mxq(z, 0, "e4m3")
    d_kb = unpack_weight(d_words, d_scales)[np.arange(K)[:, None], runs(kb, K)]
    h = 0.0625 * (d_ka.T @ zq + d_kb.T @ zq)
    nw = 0.5 * h
    ph = np.zeros((H, U))
    ph[:, unstriped(n3)] = h
    pg = ph.copy()
    pg[:, unstriped(n4)] = nw
    return pg - pg[:, unstriped(n5)]

@@ -1,0 +1,211 @@
+from contextlib import ExitStack
+
+import concourse.mybir as mybir
+
+K, T, S, H, G, U = 512, 2048, 256, 512, 2048, 512
+FLOPS = 2 * K * H * S * 3
+
+F32 = mybir.dt.float32
+BF16 = mybir.dt.bfloat16
+I32 = mybir.dt.int32
+U32 = mybir.dt.uint32
+U16 = mybir.dt.uint16
+U8 = mybir.dt.uint8
+FP8X4 = mybir.dt.float8_e4m3fn_x4
+ALU = mybir.AluOpType
+COPY = mybir.ActivationFunctionType.Copy
+
+P = 128
+PACK = 4
+HALF = S // 2
+PIECE = 256
+
+
+def entries(lst, first, count):
+    return lst[:, first // 16 : (first + count) // 16]
+
+
+def tile_picked_daqunderpagtwo_none_p_kernel(
+    tc, x_words, x_scales, w1, gs, d_words, d_scales, offs, n1, n2, ka, kb, n3, n4, n5, out
+):
+    nc = tc.nc
+    with ExitStack() as ctx:
+        keep = ctx.enter_context(tc.tile_pool(name="keep", bufs=1))
+        psum = ctx.enter_context(tc.psum_pool(name="psum", bufs=1))
+
+        def sb(name, shape, dtype, tag=""):
+            return keep.tile(shape, dtype, name=name, tag=tag, align_bytes=64)
+
+        def load_list(name, src):
+            lst = keep.tile(list(src.shape), U16, name=name)
+            nc.sync.dma_start(lst[:], src)
+            return lst
+
+        x_byte_table = sb("x_byte_table", [P, T], U8)
+        d_byte_table = sb("d_byte_table", [P, G], U8)
+        d_plane = sb("d_plane", [P, 2 * H], U8)
+        w_rows = w1.rearrange("(p j) c -> p j c", j=PACK)
+        w_raw = [sb("w_raw%d" % u, [P, PACK, H // 2], F32) for u in range(2)]
+        x_word_table = sb("x_word_table", [P, T], I32)
+        d_word_table = sb("d_word_table", [P, G], I32)
+        gain = sb("gain", [P, PACK], F32)
+        nc.gpsimd.memset(d_byte_table[:].bitcast(I32), 0)
+        nc.gpsimd.dma_start(d_byte_table[0:P:8, :].bitcast(I32), d_scales[0].bitcast(I32))
+        nc.gpsimd.dma_start(gain[:], gs.rearrange("(p t) o -> p (t o)", t=PACK))
+        nc.vector.memset(d_plane[:].bitcast(I32), 0)
+        offs_sb = load_list("offs_sb", offs)
+        ka_sb = load_list("ka_sb", ka)
+        nc.sync.dma_start(w_raw[0][:], w_rows[:, :, 0 : H // 2])
+        for q in range(4):
+            nc.sync.dma_start(
+                x_byte_table[32 * q : 32 * (q + 1), :].bitcast(I32),
+                x_scales[0][4 * q : 4 * (q + 1), :].bitcast(I32).partition_broadcast(8),
+            )
+        nc.sync.dma_start(w_raw[1][:], w_rows[:, :, H // 2 : H])
+        kb_sb = load_list("kb_sb", kb)
+        nc.sync.dma_start(x_word_table[:], x_words[0].rearrange("p n r -> p (n r)").bitcast(I32))
+        n1_sb = load_list("n1_sb", n1)
+        n2_sb = load_list("n2_sb", n2)
+        nc.sync.dma_start(d_word_table[:], d_words[0].rearrange("p n r -> p (n r)").bitcast(I32))
+        n3_sb = load_list("n3_sb", n3)
+        n4_sb = load_list("n4_sb", n4)
+        n5_sb = load_list("n5_sb", n5)
+
+        neg_gain = sb("neg_gain", [P, PACK], F32)
+        nc.gpsimd.tensor_scalar(neg_gain[:], gain[:], -1.0, 0.0, ALU.mult, ALU.add)
+
+        w_bf = sb("w_bf", [P, PACK, P, PACK], BF16)
+        w_codes = sb("w_codes", [P, H], U32, tag="d_codes")
+        w_plane = sb("w_plane", [P, H], U8)
+        w_walk = w_bf[:].rearrange("p t m j -> p m t j")
+        w_src = [raw[:].rearrange("p j (m t) -> p m t j", t=PACK) for raw in w_raw]
+        nc.scalar.activation(w_walk[:, 0:64], w_src[0], COPY)
+        nc.vector.tensor_copy(w_walk[:, 64:96], w_src[1][:, 0:32])
+        nc.scalar.activation(w_walk[:, 96:128], w_src[1][:, 32:64], COPY)
+        for t in range(PACK):
+            cols = slice(t * P, (t + 1) * P)
+            nc.vector.quantize_mx(
+                out=w_codes[:, cols].bitcast(FP8X4),
+                scales=w_plane[:, cols],
+                in_=w_bf[:, t].rearrange("p m j -> p (m j)"),
+            )
+
+        x_codes = sb("x_codes", [P, S], U32)
+        x_plane = sb("x_plane", [P, S], U8)
+        nc.vector.tensor_copy(x_plane[:], x_byte_table[:].indirect(offs_sb[:]))
+        nc.vector.tensor_copy(x_codes[:], x_word_table[:].bitcast(U32).indirect(offs_sb[:]))
+
+        y_sb = [sb("y_sb%d" % t, [P, S], F32) for t in range(PACK)]
+        gy = sb("gy", [P, PACK, S], F32)
+        for t in range(PACK):
+            cols = slice(t * P, (t + 1) * P)
+            y_ps = psum.tile([P, S], F32, name="bank%d" % t)
+            nc.tensor.matmul_mx(
+                y_ps[:], lhsT=w_codes[:, cols].bitcast(FP8X4), lhsT_scale=w_plane[:, cols],
+                rhs=x_codes[:].bitcast(FP8X4), rhs_scale=x_plane[:], start=True, stop=True,
+            )
+            if t == 0:
+                nc.scalar.activation(y_sb[t][:], y_ps[:], COPY)
+            else:
+                nc.vector.tensor_copy(y_sb[t][:], y_ps[:])
+            nc.gpsimd.tensor_scalar(gy[:, t, :], y_sb[t][:], gain[:, t : t + 1], 0.0, ALU.mult, ALU.add)
+
+        d_bytes = sb("d_bytes", [P, 2 * H], U8)
+        for which, lst in enumerate((ka_sb, kb_sb)):
+            for first in range(0, H, PIECE):
+                at = which * H + first
+                nc.vector.tensor_copy(d_bytes[:, at : at + PIECE], d_byte_table[:].indirect(entries(lst, first, PIECE)))
+        for r in range(4):
+            nc.sync.dma_start(d_plane[r:P:32, :].bitcast(I32), d_bytes[8 * r : P : 32, :].bitcast(I32))
+
+        def gather_d_words(first):
+            d_codes = sb("d_codes%d" % first, [P, 2, PIECE], U32, tag="d_codes")
+            for which, lst in enumerate((ka_sb, kb_sb)):
+                nc.vector.tensor_copy(
+                    d_codes[:, which, :], d_word_table[:].bitcast(U32).indirect(entries(lst, first, PIECE))
+                )
+            return d_codes
+
+        z_codes = sb("z_codes", [P, S], U32)
+        z_plane = sb("z_plane", [P, S], U8)
+
+        def make_z(half):
+            first = half * HALF
+            cols = slice(first, first + HALF)
+            y_n1 = sb("y_n1_%d" % half, [P, PACK, HALF], F32)
+            y_n2 = sb("y_n2_%d" % half, [P, PACK, HALF], F32)
+            low = sb("low%d" % half, [P, PACK, HALF], F32, tag="relay%d" % half)
+            z32 = sb("z32_%d" % half, [P, PACK, HALF], F32)
+            z_bf = sb("z_bf%d" % half, [P, HALF, PACK], BF16, tag="relay%d" % (half + 1))
+            for t in range(PACK):
+                nc.scalar.activation(y_n1[:, t, :], y_sb[t][:].indirect(entries(n1_sb, first, HALF)), COPY)
+                nc.scalar.activation(y_n2[:, t, :], y_sb[t][:].indirect(entries(n2_sb, first, HALF)), COPY)
+                nc.vector.tensor_tensor(low[:, t, :], y_n1[:, t, :], y_n2[:, t, :], ALU.min)
+                nc.vector.scalar_tensor_tensor(
+                    z32[:, t, :], low[:, t, :], neg_gain[:, t : t + 1], gy[:, t, cols], ALU.mult, ALU.add
+                )
+            nc.vector.tensor_copy(
+                z_bf[:].rearrange("p (c i) t -> p c t i", i=4), z32[:].rearrange("p t (c i) -> p c t i", i=4)
+            )
+            nc.vector.quantize_mx(
+                out=z_codes[:, cols].bitcast(FP8X4), scales=z_plane[:, cols],
+                in_=z_bf[:].rearrange("p j t -> p (j t)"),
+            )
+
+        h_sb = [sb("h_sb%d" % b, [P, S], F32) for b in range(4)]
+        page = [sb("page%d" % b, [P, U], F32) for b in range(4)]
+
+        def make_h(b, d_codes, first, count, bank):
+            cols = slice(first, first + count)
+            h_ps = psum.tile([P, count], F32, name=bank)
+            for which in range(2):
+                rows = slice(which * H + b * P, which * H + (b + 1) * P)
+                nc.tensor.matmul_mx(
+                    h_ps[:], lhsT=d_codes[:, which, (b % 2) * P : (b % 2 + 1) * P].bitcast(FP8X4), lhsT_scale=d_plane[:, rows],
+                    rhs=z_codes[:, cols].bitcast(FP8X4), rhs_scale=z_plane[:, cols],
+                    start=(which == 0), stop=(which == 1),
+                )
+            nc.vector.tensor_scalar(h_sb[b][:, cols], h_ps[:], 0.0625, None, ALU.mult)
+
+        def put(b, lst, factor, first, count):
+            nc.scalar.activation(
+                page[b][:].indirect(entries(lst, first, count)), h_sb[b][:, first : first + count], COPY, scale=factor
+            )
+
+        def finish(b, first, count):
+            cols = slice(first, first + count)
+            looked = sb("looked%d_%d" % (b, first), [P, count], F32)
+            result = sb("result%d_%d" % (b, first), [P, count], F32)
+            nc.scalar.activation(looked[:], page[b][:].indirect(entries(n5_sb, first, count)), COPY)
+            nc.vector.tensor_tensor(result[:], page[b][:, cols], looked[:], ALU.subtract)
+            nc.sync.dma_start(out[b * P : (b + 1) * P, cols], result[:])
+
+        make_z(0)
+        d_codes = gather_d_words(0)
+        for b in range(2):
+            make_h(b, d_codes, 0, HALF, "bank%d" % (4 + b))
+        make_z(1)
+        for lst, factor in ((n3_sb, 1.0), (n4_sb, 0.5)):
+            for b in range(2):
+                put(b, lst, factor, 0, HALF)
+        for b in range(2):
+            make_h(b, d_codes, HALF, HALF, "bank%d" % (6 + b))
+        d_codes = gather_d_words(PIECE)
+        for b in range(2, 4):
+            make_h(b, d_codes, 0, S, "bank%d" % (b - 2))
+        for lst, factor in ((n3_sb, 1.0), (n4_sb, 0.5)):
+            for b in range(2):
+                put(b, lst, factor, HALF, HALF)
+        put(2, n3_sb, 1.0, 0, S)
+        finish(0, 0, 256)
+        finish(0, 256, 256)
+        put(2, n4_sb, 0.5, 0, S)
+        finish(1, 0, 256)
+        put(3, n3_sb, 1.0, 0, S)
+        finish(1, 256, 256)
+        finish(2, 0, 256)
+        put(3, n4_sb, 0.5, 0, S)
+        finish(2, 256, 256)
+        finish(3, 0, 256)
+        finish(3, 256, 128)
+        finish(3, 384, 128)

@@ -42,7 +42,7 @@ def tile_picked_daqunderpagtwo_none_p_kernel(
             return lst
 
         x_byte_table = sb("x_byte_table", [P, T], U8)
-        d_byte_table = sb("d_byte_table", [P, G], U8)
+        d_byte_table = sb("d_byte_table", [P, G], U8, tag="d_byte_table")
         d_plane = sb("d_plane", [P, 2 * H], U8)
         w_rows = w1.rearrange("(p j) c -> p j c", j=PACK)
         w_raw = [sb("w_raw%d" % u, [P, PACK, H // 2], F32) for u in range(2)]
@@ -50,22 +50,22 @@ def tile_picked_daqunderpagtwo_none_p_kernel(
         d_word_table = sb("d_word_table", [P, G], I32)
         gain = sb("gain", [P, PACK], F32)
         nc.gpsimd.memset(d_byte_table[:].bitcast(I32), 0)
-        nc.gpsimd.dma_start(d_byte_table[0:P:8, :].bitcast(I32), d_scales[0].bitcast(I32))
-        nc.gpsimd.dma_start(gain[:], gs.rearrange("(p t) o -> p (t o)", t=PACK))
-        nc.vector.memset(d_plane[:].bitcast(I32), 0)
+        nc.gpsimd.memset(d_plane[:].bitcast(I32), 0)
         offs_sb = load_list("offs_sb", offs)
         ka_sb = load_list("ka_sb", ka)
-        nc.sync.dma_start(w_raw[0][:], w_rows[:, :, 0 : H // 2])
+        kb_sb = load_list("kb_sb", kb)
+        nc.scalar.dma_start(d_byte_table[0:P:8, :].bitcast(I32), d_scales[0].bitcast(I32))
+        for u in range(2):
+            nc.sync.dma_start(w_raw[u][:], w_rows[:, :, u * (H // 2) : (u + 1) * (H // 2)])
         for q in range(4):
             nc.sync.dma_start(
                 x_byte_table[32 * q : 32 * (q + 1), :].bitcast(I32),
                 x_scales[0][4 * q : 4 * (q + 1), :].bitcast(I32).partition_broadcast(8),
             )
-        nc.sync.dma_start(w_raw[1][:], w_rows[:, :, H // 2 : H])
-        kb_sb = load_list("kb_sb", kb)
         nc.sync.dma_start(x_word_table[:], x_words[0].rearrange("p n r -> p (n r)").bitcast(I32))
         n1_sb = load_list("n1_sb", n1)
         n2_sb = load_list("n2_sb", n2)
+        nc.sync.dma_start(gain[:], gs.rearrange("(p t) o -> p (t o)", t=PACK))
         nc.sync.dma_start(d_word_table[:], d_words[0].rearrange("p n r -> p (n r)").bitcast(I32))
         n3_sb = load_list("n3_sb", n3)
         n4_sb = load_list("n4_sb", n4)
@@ -74,24 +74,27 @@ def tile_picked_daqunderpagtwo_none_p_kernel(
         neg_gain = sb("neg_gain", [P, PACK], F32)
         nc.gpsimd.tensor_scalar(neg_gain[:], gain[:], -1.0, 0.0, ALU.mult, ALU.add)
 
-        w_bf = sb("w_bf", [P, PACK, P, PACK], BF16)
+        w_bf = sb("w_bf", [P, PACK, P, PACK], BF16, tag="w_bf")
         w_codes = sb("w_codes", [P, H], U32, tag="d_codes")
         w_plane = sb("w_plane", [P, H], U8)
         w_walk = w_bf[:].rearrange("p t m j -> p m t j")
         w_src = [raw[:].rearrange("p j (m t) -> p m t j", t=PACK) for raw in w_raw]
-        nc.scalar.activation(w_walk[:, 0:64], w_src[0], COPY)
-        nc.vector.tensor_copy(w_walk[:, 64:96], w_src[1][:, 0:32])
-        nc.scalar.activation(w_walk[:, 96:128], w_src[1][:, 32:64], COPY)
-        for t in range(PACK):
-            cols = slice(t * P, (t + 1) * P)
-            nc.vector.quantize_mx(
-                out=w_codes[:, cols].bitcast(FP8X4),
-                scales=w_plane[:, cols],
-                in_=w_bf[:, t].rearrange("p m j -> p (m j)"),
-            )
+        for u in range(2):
+            nc.scalar.activation(w_walk[:, 64 * u : 64 * (u + 1)], w_src[u], COPY)
+        nc.vector.quantize_mx(
+            out=w_codes[:].bitcast(FP8X4), scales=w_plane[:], in_=w_bf[:].rearrange("p t m j -> p (t m j)")
+        )
 
-        x_codes = sb("x_codes", [P, S], U32)
-        x_plane = sb("x_plane", [P, S], U8)
+        d_bytes = sb("d_bytes", [P, 2 * H], U8)
+        for which, lst in enumerate((ka_sb, kb_sb)):
+            for first in range(0, H, PIECE):
+                at = which * H + first
+                nc.vector.tensor_copy(d_bytes[:, at : at + PIECE], d_byte_table[:].indirect(entries(lst, first, PIECE)))
+        for r in range(4):
+            nc.sync.dma_start(d_plane[r:P:32, :].bitcast(I32), d_bytes[8 * r : P : 32, :].bitcast(I32))
+
+        x_codes = sb("x_codes", [P, S], U32, tag="w_bf")
+        x_plane = sb("x_plane", [P, S], U8, tag="d_byte_table")
         nc.vector.tensor_copy(x_plane[:], x_byte_table[:].indirect(offs_sb[:]))
         nc.vector.tensor_copy(x_codes[:], x_word_table[:].bitcast(U32).indirect(offs_sb[:]))
 
@@ -104,19 +107,11 @@ def tile_picked_daqunderpagtwo_none_p_kernel(
                 y_ps[:], lhsT=w_codes[:, cols].bitcast(FP8X4), lhsT_scale=w_plane[:, cols],
                 rhs=x_codes[:].bitcast(FP8X4), rhs_scale=x_plane[:], start=True, stop=True,
             )
-            if t == 0:
+            if t < 3:
                 nc.scalar.activation(y_sb[t][:], y_ps[:], COPY)
             else:
                 nc.vector.tensor_copy(y_sb[t][:], y_ps[:])
             nc.gpsimd.tensor_scalar(gy[:, t, :], y_sb[t][:], gain[:, t : t + 1], 0.0, ALU.mult, ALU.add)
-
-        d_bytes = sb("d_bytes", [P, 2 * H], U8)
-        for which, lst in enumerate((ka_sb, kb_sb)):
-            for first in range(0, H, PIECE):
-                at = which * H + first
-                nc.vector.tensor_copy(d_bytes[:, at : at + PIECE], d_byte_table[:].indirect(entries(lst, first, PIECE)))
-        for r in range(4):
-            nc.sync.dma_start(d_plane[r:P:32, :].bitcast(I32), d_bytes[8 * r : P : 32, :].bitcast(I32))
 
         def gather_d_words(first):
             d_codes = sb("d_codes%d" % first, [P, 2, PIECE], U32, tag="d_codes")
@@ -140,7 +135,11 @@ def tile_picked_daqunderpagtwo_none_p_kernel(
             for t in range(PACK):
                 nc.scalar.activation(y_n1[:, t, :], y_sb[t][:].indirect(entries(n1_sb, first, HALF)), COPY)
                 nc.scalar.activation(y_n2[:, t, :], y_sb[t][:].indirect(entries(n2_sb, first, HALF)), COPY)
-                nc.vector.tensor_tensor(low[:, t, :], y_n1[:, t, :], y_n2[:, t, :], ALU.min)
+                if half == 0:
+                    nc.vector.tensor_tensor(low[:, t, :], y_n1[:, t, :], y_n2[:, t, :], ALU.min)
+            if half == 1:
+                nc.vector.tensor_tensor(low[:], y_n1[:], y_n2[:], ALU.min)
+            for t in range(PACK):
                 nc.vector.scalar_tensor_tensor(
                     z32[:, t, :], low[:, t, :], neg_gain[:, t : t + 1], gy[:, t, cols], ALU.mult, ALU.add
                 )

@@ -47,21 +47,19 @@ def tile_picked_daqunderpagtwo_none_p_kernel(
         w_rows = w1.rearrange("(p j) c -> p j c", j=PACK)
         w_raw = [sb("w_raw%d" % u, [P, PACK, H // 2], F32) for u in range(2)]
         x_word_table = sb("x_word_table", [P, T], I32)
-        d_word_table = sb("d_word_table", [P, G], I32)
-        gain = sb("gain", [P, PACK], F32)
+        d_word_table = sb("d_word_table", [P, G], I32, tag="relay0")
+        gain = sb("gain", [P, PACK], F32, tag="gain")
         nc.gpsimd.memset(d_byte_table[:].bitcast(I32), 0)
+        nc.vector.memset(x_byte_table[:].bitcast(I32), 0)
         nc.gpsimd.memset(d_plane[:].bitcast(I32), 0)
         offs_sb = load_list("offs_sb", offs)
         ka_sb = load_list("ka_sb", ka)
         kb_sb = load_list("kb_sb", kb)
-        nc.scalar.dma_start(d_byte_table[0:P:8, :].bitcast(I32), d_scales[0].bitcast(I32))
+        nc.sync.dma_start(d_byte_table[0:P:8, :].bitcast(I32), d_scales[0].bitcast(I32))
         for u in range(2):
             nc.sync.dma_start(w_raw[u][:], w_rows[:, :, u * (H // 2) : (u + 1) * (H // 2)])
-        for q in range(4):
-            nc.sync.dma_start(
-                x_byte_table[32 * q : 32 * (q + 1), :].bitcast(I32),
-                x_scales[0][4 * q : 4 * (q + 1), :].bitcast(I32).partition_broadcast(8),
-            )
+        for r in range(4):
+            nc.sync.dma_start(x_byte_table[r:P:32, :].bitcast(I32), x_scales[0][r:16:4, :].bitcast(I32))
         nc.sync.dma_start(x_word_table[:], x_words[0].rearrange("p n r -> p (n r)").bitcast(I32))
         n1_sb = load_list("n1_sb", n1)
         n2_sb = load_list("n2_sb", n2)
@@ -107,19 +105,19 @@ def tile_picked_daqunderpagtwo_none_p_kernel(
                 y_ps[:], lhsT=w_codes[:, cols].bitcast(FP8X4), lhsT_scale=w_plane[:, cols],
                 rhs=x_codes[:].bitcast(FP8X4), rhs_scale=x_plane[:], start=True, stop=True,
             )
-            if t < 3:
+            if t < 2:
                 nc.scalar.activation(y_sb[t][:], y_ps[:], COPY)
             else:
                 nc.vector.tensor_copy(y_sb[t][:], y_ps[:])
             nc.gpsimd.tensor_scalar(gy[:, t, :], y_sb[t][:], gain[:, t : t + 1], 0.0, ALU.mult, ALU.add)
 
-        def gather_d_words(first):
-            d_codes = sb("d_codes%d" % first, [P, 2, PIECE], U32, tag="d_codes")
+        d_codes = sb("d_codes", [P, 2 * H], U32, tag="d_codes")
+        for first in range(0, H, PIECE):
             for which, lst in enumerate((ka_sb, kb_sb)):
+                at = which * H + first
                 nc.vector.tensor_copy(
-                    d_codes[:, which, :], d_word_table[:].bitcast(U32).indirect(entries(lst, first, PIECE))
+                    d_codes[:, at : at + PIECE], d_word_table[:].bitcast(U32).indirect(entries(lst, first, PIECE))
                 )
-            return d_codes
 
         z_codes = sb("z_codes", [P, S], U32)
         z_plane = sb("z_plane", [P, S], U8)
@@ -127,18 +125,17 @@ def tile_picked_daqunderpagtwo_none_p_kernel(
         def make_z(half):
             first = half * HALF
             cols = slice(first, first + HALF)
-            y_n1 = sb("y_n1_%d" % half, [P, PACK, HALF], F32)
-            y_n2 = sb("y_n2_%d" % half, [P, PACK, HALF], F32)
+            picked = sb("picked%d" % half, [P, 2, PACK, HALF], F32, tag=("picked", "gain")[half])
             low = sb("low%d" % half, [P, PACK, HALF], F32, tag="relay%d" % half)
             z32 = sb("z32_%d" % half, [P, PACK, HALF], F32)
             z_bf = sb("z_bf%d" % half, [P, HALF, PACK], BF16, tag="relay%d" % (half + 1))
             for t in range(PACK):
-                nc.scalar.activation(y_n1[:, t, :], y_sb[t][:].indirect(entries(n1_sb, first, HALF)), COPY)
-                nc.scalar.activation(y_n2[:, t, :], y_sb[t][:].indirect(entries(n2_sb, first, HALF)), COPY)
+                nc.scalar.activation(picked[:, 0, t, :], y_sb[t][:].indirect(entries(n1_sb, first, HALF)), COPY)
+                nc.scalar.activation(picked[:, 1, t, :], y_sb[t][:].indirect(entries(n2_sb, first, HALF)), COPY)
                 if half == 0:
-                    nc.vector.tensor_tensor(low[:, t, :], y_n1[:, t, :], y_n2[:, t, :], ALU.min)
+                    nc.vector.tensor_tensor(low[:, t, :], picked[:, 0, t, :], picked[:, 1, t, :], ALU.min)
             if half == 1:
-                nc.vector.tensor_tensor(low[:], y_n1[:], y_n2[:], ALU.min)
+                nc.vector.tensor_tensor(low[:], picked[:, 0], picked[:, 1], ALU.min)
             for t in range(PACK):
                 nc.vector.scalar_tensor_tensor(
                     z32[:, t, :], low[:, t, :], neg_gain[:, t : t + 1], gy[:, t, cols], ALU.mult, ALU.add
@@ -154,17 +151,20 @@ def tile_picked_daqunderpagtwo_none_p_kernel(
         h_sb = [sb("h_sb%d" % b, [P, S], F32) for b in range(4)]
         page = [sb("page%d" % b, [P, U], F32) for b in range(4)]
 
-        def make_h(b, d_codes, first, count, bank):
+        def make_h(b, first, count, bank):
             cols = slice(first, first + count)
             h_ps = psum.tile([P, count], F32, name=bank)
             for which in range(2):
                 rows = slice(which * H + b * P, which * H + (b + 1) * P)
                 nc.tensor.matmul_mx(
-                    h_ps[:], lhsT=d_codes[:, which, (b % 2) * P : (b % 2 + 1) * P].bitcast(FP8X4), lhsT_scale=d_plane[:, rows],
+                    h_ps[:], lhsT=d_codes[:, rows].bitcast(FP8X4), lhsT_scale=d_plane[:, rows],
                     rhs=z_codes[:, cols].bitcast(FP8X4), rhs_scale=z_plane[:, cols],
                     start=(which == 0), stop=(which == 1),
                 )
-            nc.vector.tensor_scalar(h_sb[b][:, cols], h_ps[:], 0.0625, None, ALU.mult)
+            if first == 0 and b < 2:
+                nc.scalar.activation(h_sb[b][:, cols], h_ps[:], COPY, scale=0.0625)
+            else:
+                nc.vector.tensor_scalar(h_sb[b][:, cols], h_ps[:], 0.0625, None, ALU.mult)
 
         def put(b, lst, factor, first, count):
             nc.scalar.activation(
@@ -180,30 +180,27 @@ def tile_picked_daqunderpagtwo_none_p_kernel(
             nc.sync.dma_start(out[b * P : (b + 1) * P, cols], result[:])
 
         make_z(0)
-        d_codes = gather_d_words(0)
-        for b in range(2):
-            make_h(b, d_codes, 0, HALF, "bank%d" % (4 + b))
+        for b in range(4):
+            make_h(b, 0, HALF, "bank%d" % (4 + b))
         make_z(1)
-        for lst, factor in ((n3_sb, 1.0), (n4_sb, 0.5)):
-            for b in range(2):
-                put(b, lst, factor, 0, HALF)
-        for b in range(2):
-            make_h(b, d_codes, HALF, HALF, "bank%d" % (6 + b))
-        d_codes = gather_d_words(PIECE)
-        for b in range(2, 4):
-            make_h(b, d_codes, 0, S, "bank%d" % (b - 2))
+        for pair in (0, 2):
+            for lst, factor in ((n3_sb, 1.0), (n4_sb, 0.5)):
+                for b in (pair, pair + 1):
+                    put(b, lst, factor, 0, HALF)
+        for b in range(4):
+            make_h(b, HALF, HALF, "bank%d" % b)
         for lst, factor in ((n3_sb, 1.0), (n4_sb, 0.5)):
             for b in range(2):
                 put(b, lst, factor, HALF, HALF)
-        put(2, n3_sb, 1.0, 0, S)
+        put(2, n3_sb, 1.0, HALF, HALF)
         finish(0, 0, 256)
+        put(2, n4_sb, 0.5, HALF, HALF)
         finish(0, 256, 256)
-        put(2, n4_sb, 0.5, 0, S)
+        put(3, n3_sb, 1.0, HALF, HALF)
         finish(1, 0, 256)
-        put(3, n3_sb, 1.0, 0, S)
+        put(3, n4_sb, 0.5, HALF, HALF)
         finish(1, 256, 256)
         finish(2, 0, 256)
-        put(3, n4_sb, 0.5, 0, S)
         finish(2, 256, 256)
         finish(3, 0, 256)
         finish(3, 256, 128)

from contextlib import ExitStack

import concourse.mybir as mybir

K, T, S, H, G, U = 512, 2048, 256, 512, 2048, 512
FLOPS = 2 * K * H * S * 3

F32 = mybir.dt.float32
BF16 = mybir.dt.bfloat16
I32 = mybir.dt.int32
U32 = mybir.dt.uint32
U16 = mybir.dt.uint16
U8 = mybir.dt.uint8
FP8X4 = mybir.dt.float8_e4m3fn_x4
ALU = mybir.AluOpType
COPY = mybir.ActivationFunctionType.Copy

P = 128
PACK = 4
HALF = S // 2
PIECE = 256


def entries(lst, first, count):
    return lst[:, first // 16 : (first + count) // 16]


def tile_picked_daqunderpagtwo_none_p_kernel(
    tc, x_words, x_scales, w1, gs, d_words, d_scales, offs, n1, n2, ka, kb, n3, n4, n5, out
):
    nc = tc.nc
    with ExitStack() as ctx:
        keep = ctx.enter_context(tc.tile_pool(name="keep", bufs=1))
        psum = ctx.enter_context(tc.psum_pool(name="psum", bufs=1))

        def sb(name, shape, dtype, tag=""):
            return keep.tile(shape, dtype, name=name, tag=tag, align_bytes=64)

        def load_list(name, src):
            lst = keep.tile(list(src.shape), U16, name=name)
            nc.sync.dma_start(lst[:], src)
            return lst

        x_byte_table = sb("x_byte_table", [P, T], U8)
        d_byte_table = sb("d_byte_table", [P, G], U8, tag="d_byte_table")
        d_plane = sb("d_plane", [P, 2 * H], U8)
        w_rows = w1.rearrange("(p j) c -> p j c", j=PACK)
        w_raw = [sb("w_raw%d" % u, [P, PACK, H // 2], F32) for u in range(2)]
        x_word_table = sb("x_word_table", [P, T], I32)
        d_word_table = sb("d_word_table", [P, G], I32, tag="relay0")
        gain = sb("gain", [P, PACK], F32, tag="gain")
        nc.gpsimd.memset(d_byte_table[:].bitcast(I32), 0)
        nc.vector.memset(x_byte_table[:].bitcast(I32), 0)
        nc.gpsimd.memset(d_plane[:].bitcast(I32), 0)
        offs_sb = load_list("offs_sb", offs)
        ka_sb = load_list("ka_sb", ka)
        kb_sb = load_list("kb_sb", kb)
        nc.sync.dma_start(d_byte_table[0:P:8, :].bitcast(I32), d_scales[0].bitcast(I32))
        for u in range(2):
            nc.sync.dma_start(w_raw[u][:], w_rows[:, :, u * (H // 2) : (u + 1) * (H // 2)])
        for r in range(4):
            nc.sync.dma_start(x_byte_table[r:P:32, :].bitcast(I32), x_scales[0][r:16:4, :].bitcast(I32))
        nc.sync.dma_start(x_word_table[:], x_words[0].rearrange("p n r -> p (n r)").bitcast(I32))
        n1_sb = load_list("n1_sb", n1)
        n2_sb = load_list("n2_sb", n2)
        nc.sync.dma_start(gain[:], gs.rearrange("(p t) o -> p (t o)", t=PACK))
        nc.sync.dma_start(d_word_table[:], d_words[0].rearrange("p n r -> p (n r)").bitcast(I32))
        n3_sb = load_list("n3_sb", n3)
        n4_sb = load_list("n4_sb", n4)
        n5_sb = load_list("n5_sb", n5)

        neg_gain = sb("neg_gain", [P, PACK], F32)
        nc.gpsimd.tensor_scalar(neg_gain[:], gain[:], -1.0, 0.0, ALU.mult, ALU.add)

        w_bf = sb("w_bf", [P, PACK, P, PACK], BF16, tag="w_bf")
        w_codes = sb("w_codes", [P, H], U32, tag="d_codes")
        w_plane = sb("w_plane", [P, H], U8)
        w_walk = w_bf[:].rearrange("p t m j -> p m t j")
        w_src = [raw[:].rearrange("p j (m t) -> p m t j", t=PACK) for raw in w_raw]
        for u in range(2):
            nc.scalar.activation(w_walk[:, 64 * u : 64 * (u + 1)], w_src[u], COPY)
        nc.vector.quantize_mx(
            out=w_codes[:].bitcast(FP8X4), scales=w_plane[:], in_=w_bf[:].rearrange("p t m j -> p (t m j)")
        )

        d_bytes = sb("d_bytes", [P, 2 * H], U8)
        for which, lst in enumerate((ka_sb, kb_sb)):
            for first in range(0, H, PIECE):
                at = which * H + first
                nc.vector.tensor_copy(d_bytes[:, at : at + PIECE], d_byte_table[:].indirect(entries(lst, first, PIECE)))
        for r in range(4):
            nc.sync.dma_start(d_plane[r:P:32, :].bitcast(I32), d_bytes[8 * r : P : 32, :].bitcast(I32))

        x_codes = sb("x_codes", [P, S], U32, tag="w_bf")
        x_plane = sb("x_plane", [P, S], U8, tag="d_byte_table")
        nc.vector.tensor_copy(x_plane[:], x_byte_table[:].indirect(offs_sb[:]))
        nc.vector.tensor_copy(x_codes[:], x_word_table[:].bitcast(U32).indirect(offs_sb[:]))

        y_sb = [sb("y_sb%d" % t, [P, S], F32) for t in range(PACK)]
        gy = sb("gy", [P, PACK, S], F32)
        for t in range(PACK):
            cols = slice(t * P, (t + 1) * P)
            y_ps = psum.tile([P, S], F32, name="bank%d" % t)
            nc.tensor.matmul_mx(
                y_ps[:], lhsT=w_codes[:, cols].bitcast(FP8X4), lhsT_scale=w_plane[:, cols],
                rhs=x_codes[:].bitcast(FP8X4), rhs_scale=x_plane[:], start=True, stop=True,
            )
            if t < 2:
                nc.scalar.activation(y_sb[t][:], y_ps[:], COPY)
            else:
                nc.vector.tensor_copy(y_sb[t][:], y_ps[:])
            nc.gpsimd.tensor_scalar(gy[:, t, :], y_sb[t][:], gain[:, t : t + 1], 0.0, ALU.mult, ALU.add)

        d_codes = sb("d_codes", [P, 2 * H], U32, tag="d_codes")
        for first in range(0, H, PIECE):
            for which, lst in enumerate((ka_sb, kb_sb)):
                at = which * H + first
                nc.vector.tensor_copy(
                    d_codes[:, at : at + PIECE], d_word_table[:].bitcast(U32).indirect(entries(lst, first, PIECE))
                )

        z_codes = sb("z_codes", [P, S], U32)
        z_plane = sb("z_plane", [P, S], U8)

        def make_z(half):
            first = half * HALF
            cols = slice(first, first + HALF)
            picked = sb("picked%d" % half, [P, 2, PACK, HALF], F32, tag=("picked", "gain")[half])
            low = sb("low%d" % half, [P, PACK, HALF], F32, tag="relay%d" % half)
            z32 = sb("z32_%d" % half, [P, PACK, HALF], F32)
            z_bf = sb("z_bf%d" % half, [P, HALF, PACK], BF16, tag="relay%d" % (half + 1))
            for t in range(PACK):
                nc.scalar.activation(picked[:, 0, t, :], y_sb[t][:].indirect(entries(n1_sb, first, HALF)), COPY)
                nc.scalar.activation(picked[:, 1, t, :], y_sb[t][:].indirect(entries(n2_sb, first, HALF)), COPY)
                if half == 0:
                    nc.vector.tensor_tensor(low[:, t, :], picked[:, 0, t, :], picked[:, 1, t, :], ALU.min)
            if half == 1:
                nc.vector.tensor_tensor(low[:], picked[:, 0], picked[:, 1], ALU.min)
            for t in range(PACK):
                nc.vector.scalar_tensor_tensor(
                    z32[:, t, :], low[:, t, :], neg_gain[:, t : t + 1], gy[:, t, cols], ALU.mult, ALU.add
                )
            nc.vector.tensor_copy(
                z_bf[:].rearrange("p (c i) t -> p c t i", i=4), z32[:].rearrange("p t (c i) -> p c t i", i=4)
            )
            nc.vector.quantize_mx(
                out=z_codes[:, cols].bitcast(FP8X4), scales=z_plane[:, cols],
                in_=z_bf[:].rearrange("p j t -> p (j t)"),
            )

        h_sb = [sb("h_sb%d" % b, [P, S], F32) for b in range(4)]
        page = [sb("page%d" % b, [P, U], F32) for b in range(4)]

        def make_h(b, first, count, bank):
            cols = slice(first, first + count)
            h_ps = psum.tile([P, count], F32, name=bank)
            for which in range(2):
                rows = slice(which * H + b * P, which * H + (b + 1) * P)
                nc.tensor.matmul_mx(
                    h_ps[:], lhsT=d_codes[:, rows].bitcast(FP8X4), lhsT_scale=d_plane[:, rows],
                    rhs=z_codes[:, cols].bitcast(FP8X4), rhs_scale=z_plane[:, cols],
                    start=(which == 0), stop=(which == 1),
                )
            if first == 0 and b < 2:
                nc.scalar.activation(h_sb[b][:, cols], h_ps[:], COPY, scale=0.0625)
            else:
                nc.vector.tensor_scalar(h_sb[b][:, cols], h_ps[:], 0.0625, None, ALU.mult)

        def put(b, lst, factor, first, count):
            nc.scalar.activation(
                page[b][:].indirect(entries(lst, first, count)), h_sb[b][:, first : first + count], COPY, scale=factor
            )

        def finish(b, first, count):
            cols = slice(first, first + count)
            looked = sb("looked%d_%d" % (b, first), [P, count], F32)
            result = sb("result%d_%d" % (b, first), [P, count], F32)
            nc.scalar.activation(looked[:], page[b][:].indirect(entries(n5_sb, first, count)), COPY)
            nc.vector.tensor_tensor(result[:], page[b][:, cols], looked[:], ALU.subtract)
            nc.sync.dma_start(out[b * P : (b + 1) * P, cols], result[:])

        make_z(0)
        for b in range(4):
            make_h(b, 0, HALF, "bank%d" % (4 + b))
        make_z(1)
        for pair in (0, 2):
            for lst, factor in ((n3_sb, 1.0), (n4_sb, 0.5)):
                for b in (pair, pair + 1):
                    put(b, lst, factor, 0, HALF)
        for b in range(4):
            make_h(b, HALF, HALF, "bank%d" % b)
        for lst, factor in ((n3_sb, 1.0), (n4_sb, 0.5)):
            for b in range(2):
                put(b, lst, factor, HALF, HALF)
        put(2, n3_sb, 1.0, HALF, HALF)
        finish(0, 0, 256)
        put(2, n4_sb, 0.5, HALF, HALF)
        finish(0, 256, 256)
        put(3, n3_sb, 1.0, HALF, HALF)
        finish(1, 0, 256)
        put(3, n4_sb, 0.5, HALF, HALF)
        finish(1, 256, 256)
        finish(2, 0, 256)
        finish(2, 256, 256)
        finish(3, 0, 256)
        finish(3, 256, 128)
        finish(3, 384, 128)
